import numpy as np
import ml_dtypes

BF16 = ml_dtypes.bfloat16


def bf(x):
    return np.asarray(x, np.float32).astype(BF16)


def f32(x):
    return np.asarray(x, np.float32)


def f64(x):
    return np.asarray(x).astype(np.float64)


def striped(idx):
    return np.tile(idx.reshape(-1, 16).T, (8, 1))


def rows(idx, k):
    return np.tile(idx, (k, 1))


def look(tab, idx):
    return np.take_along_axis(f64(tab), rows(idx, len(tab)), axis=1)


K, S, V, N, M = 256, 2048, 512, 512, 128


def silu(v):
    return v / (1.0 + np.exp(-v))


def setup_inputs():
    return {"tab": f32(np.random.standard_normal((2, K, S))), "y": f32(np.random.standard_normal((K, V))), "w": bf(np.random.standard_normal((K, M)) / np.sqrt(K)), "b": f32(0.5 * np.random.standard_normal((M, 1))), "offs": striped(np.random.permutation(S)[:N])}


def reference(tab, y, w, b, offs):
    idx = offs[:16].T.reshape(-1)
    x = (look(tab[0], idx) + f64(y)) * (silu(look(tab[1], idx)))
    return np.maximum(f64(w).T @ x + f64(b), 0.0)

@@ -1,0 +1,49 @@
+import concourse.mybir as mybir
+
+F32, BF16, U16 = mybir.dt.float32, mybir.dt.bfloat16, mybir.dt.uint16
+ADD, MULT = mybir.AluOpType.add, mybir.AluOpType.mult
+SILU, RELU = mybir.ActivationFunctionType.Silu, mybir.ActivationFunctionType.Relu
+
+P = 128
+K, S, N, M = 256, 2048, 512, 128
+BLOCKS = K // P
+FLOPS = 2 * K * N * M
+
+
+def tile_lookup_vg_addsilu_relu_kernel(tc, tab, y, w, b, offs, out):
+    nc = tc.nc
+    with (
+        tc.tile_pool(name="held", bufs=1) as held,
+        tc.psum_pool(name="psum", bufs=1) as psum,
+    ):
+        offsets = held.tile([P, N // 16], U16, name="offsets")
+        nc.sync.dma_start(offsets[:], offs)
+
+        weights = held.tile([P, BLOCKS, M], BF16, name="weights")
+        bias = held.tile([P, 1], F32, name="bias")
+        streams, gates, values = [], [], []
+        for t in range(BLOCKS):
+            streams.append(held.tile([P, N], F32, name=f"stream{t}"))
+            gates.append(held.tile([P, S], F32, name=f"gates{t}"))
+            values.append(held.tile([P, S], F32, name=f"values{t}"))
+        for t in range(BLOCKS):
+            rows = slice(t * P, (t + 1) * P)
+            nc.scalar.dma_start(streams[t][:], y[rows, :])
+            nc.sync.dma_start(gates[t][:], tab[1, rows, :])
+            nc.sync.dma_start(values[t][:], tab[0, rows, :])
+        nc.scalar.dma_start(weights[:], w.rearrange("(t p) m -> p t m", p=P))
+        nc.scalar.dma_start(bias[:], b)
+
+        product = psum.tile([M, N], F32, name="product")
+        for t in range(BLOCKS):
+            gate = held.tile([P, N], F32, name=f"gate{t}")
+            total = held.tile([P, N], F32, name=f"total{t}")
+            x = held.tile([P, N], BF16, name=f"x{t}")
+            nc.scalar.activation(gate[:], gates[t][:].indirect(offsets[:]), SILU)
+            nc.vector.tensor_tensor(total[:], values[t][:].indirect(offsets[:]), streams[t][:], ADD)
+            nc.vector.tensor_tensor(x[:], total[:], gate[:], MULT)
+            nc.tensor.matmul(product[:], weights[:, t, :], x[:], start=t == 0, stop=t == BLOCKS - 1)
+
+        result = held.tile([M, N], F32, name="result")
+        nc.scalar.activation(result[:], product[:], RELU, bias=bias[:])
+        nc.sync.dma_start(out, result[:])

@@ -7,6 +7,8 @@ SILU, RELU = mybir.ActivationFunctionType.Silu, mybir.ActivationFunctionType.Rel
 P = 128
 K, S, N, M = 256, 2048, 512, 128
 BLOCKS = K // P
+PIECES = 2
+PIECE = N // PIECES
 FLOPS = 2 * K * N * M
 
 
@@ -34,16 +36,19 @@ def tile_lookup_vg_addsilu_relu_kernel(tc, tab, y, w, b, offs, out):
         nc.scalar.dma_start(weights[:], w.rearrange("(t p) m -> p t m", p=P))
         nc.scalar.dma_start(bias[:], b)
 
-        product = psum.tile([M, N], F32, name="product")
+        products = [psum.tile([M, PIECE], F32, name=f"product{c}") for c in range(PIECES)]
+        results = [held.tile([M, PIECE], F32, name=f"result{c}") for c in range(PIECES)]
         for t in range(BLOCKS):
             gate = held.tile([P, N], F32, name=f"gate{t}")
             total = held.tile([P, N], F32, name=f"total{t}")
             x = held.tile([P, N], BF16, name=f"x{t}")
             nc.scalar.activation(gate[:], gates[t][:].indirect(offsets[:]), SILU)
-            nc.vector.tensor_tensor(total[:], values[t][:].indirect(offsets[:]), streams[t][:], ADD)
-            nc.vector.tensor_tensor(x[:], total[:], gate[:], MULT)
-            nc.tensor.matmul(product[:], weights[:, t, :], x[:], start=t == 0, stop=t == BLOCKS - 1)
-
-        result = held.tile([M, N], F32, name="result")
-        nc.scalar.activation(result[:], product[:], RELU, bias=bias[:])
-        nc.sync.dma_start(out, result[:])
+            for c in range(PIECES):
+                cols = slice(c * PIECE, (c + 1) * PIECE)
+                part = offsets[:, c * PIECE // 16 : (c + 1) * PIECE // 16]
+                nc.vector.tensor_tensor(total[:, cols], values[t][:].indirect(part), streams[t][:, cols], ADD)
+                nc.vector.tensor_tensor(x[:, cols], total[:, cols], gate[:, cols], MULT)
+                nc.tensor.matmul(products[c][:], weights[:, t, :], x[:, cols], start=t == 0, stop=t == BLOCKS - 1)
+        for c in range(PIECES):
+            nc.scalar.activation(results[c][:], products[c][:], RELU, bias=bias[:])
+            nc.sync.dma_start(out[:, c * PIECE : (c + 1) * PIECE], results[c][:])

@@ -7,7 +7,7 @@ SILU, RELU = mybir.ActivationFunctionType.Silu, mybir.ActivationFunctionType.Rel
 P = 128
 K, S, N, M = 256, 2048, 512, 128
 BLOCKS = K // P
-PIECES = 2
+PIECES = 4
 PIECE = N // PIECES
 FLOPS = 2 * K * N * M
 
@@ -38,17 +38,23 @@ def tile_lookup_vg_addsilu_relu_kernel(tc, tab, y, w, b, offs, out):
 
         products = [psum.tile([M, PIECE], F32, name=f"product{c}") for c in range(PIECES)]
         results = [held.tile([M, PIECE], F32, name=f"result{c}") for c in range(PIECES)]
+        columns = [slice(c * PIECE, (c + 1) * PIECE) for c in range(PIECES)]
         for t in range(BLOCKS):
             gate = held.tile([P, N], F32, name=f"gate{t}")
-            total = held.tile([P, N], F32, name=f"total{t}")
-            x = held.tile([P, N], BF16, name=f"x{t}")
+            totals = [held.tile([P, PIECE], F32, name=f"total{t}_{c}") for c in range(PIECES)]
             nc.scalar.activation(gate[:], gates[t][:].indirect(offsets[:]), SILU)
-            for c in range(PIECES):
-                cols = slice(c * PIECE, (c + 1) * PIECE)
+
+            def look_up(c):
                 part = offsets[:, c * PIECE // 16 : (c + 1) * PIECE // 16]
-                nc.vector.tensor_tensor(total[:, cols], values[t][:].indirect(part), streams[t][:, cols], ADD)
-                nc.vector.tensor_tensor(x[:, cols], total[:, cols], gate[:, cols], MULT)
-                nc.tensor.matmul(products[c][:], weights[:, t, :], x[:, cols], start=t == 0, stop=t == BLOCKS - 1)
+                nc.vector.tensor_tensor(totals[c][:], values[t][:].indirect(part), streams[t][:, columns[c]], ADD)
+
+            look_up(0)
+            for c in range(PIECES):
+                if c + 1 < PIECES:
+                    look_up(c + 1)
+                x = held.tile([P, PIECE], BF16, name=f"x{t}_{c}")
+                nc.vector.tensor_tensor(x[:], totals[c][:], gate[:, columns[c]], MULT)
+                nc.tensor.matmul(products[c][:], weights[:, t, :], x[:], start=t == 0, stop=t == BLOCKS - 1)
         for c in range(PIECES):
             nc.scalar.activation(results[c][:], products[c][:], RELU, bias=bias[:])
-            nc.sync.dma_start(out[:, c * PIECE : (c + 1) * PIECE], results[c][:])
+            nc.sync.dma_start(out[:, columns[c]], results[c][:])

@@ -30,11 +30,13 @@ def tile_lookup_vg_addsilu_relu_kernel(tc, tab, y, w, b, offs, out):
             values.append(held.tile([P, S], F32, name=f"values{t}"))
         for t in range(BLOCKS):
             rows = slice(t * P, (t + 1) * P)
-            nc.scalar.dma_start(streams[t][:], y[rows, :])
+            early = N if t < BLOCKS - 1 else N // 2
+            nc.scalar.dma_start(streams[t][:, :early], y[rows, :early])
             nc.sync.dma_start(gates[t][:], tab[1, rows, :])
             nc.sync.dma_start(values[t][:], tab[0, rows, :])
-        nc.scalar.dma_start(weights[:], w.rearrange("(t p) m -> p t m", p=P))
-        nc.scalar.dma_start(bias[:], b)
+        nc.sync.dma_start(weights[:], w.rearrange("(t p) m -> p t m", p=P))
+        nc.sync.dma_start(streams[-1][:, N // 2 :], y[K - P :, N // 2 :])
+        nc.sync.dma_start(bias[:], b)
 
         products = [psum.tile([M, PIECE], F32, name=f"product{c}") for c in range(PIECES)]
         results = [held.tile([M, PIECE], F32, name=f"result{c}") for c in range(PIECES)]

import concourse.mybir as mybir

F32, BF16, U16 = mybir.dt.float32, mybir.dt.bfloat16, mybir.dt.uint16
ADD, MULT = mybir.AluOpType.add, mybir.AluOpType.mult
SILU, RELU = mybir.ActivationFunctionType.Silu, mybir.ActivationFunctionType.Relu

P = 128
K, S, N, M = 256, 2048, 512, 128
BLOCKS = K // P
PIECES = 4
PIECE = N // PIECES
FLOPS = 2 * K * N * M


def tile_lookup_vg_addsilu_relu_kernel(tc, tab, y, w, b, offs, out):
    nc = tc.nc
    with (
        tc.tile_pool(name="held", bufs=1) as held,
        tc.psum_pool(name="psum", bufs=1) as psum,
    ):
        offsets = held.tile([P, N // 16], U16, name="offsets")
        nc.sync.dma_start(offsets[:], offs)

        weights = held.tile([P, BLOCKS, M], BF16, name="weights")
        bias = held.tile([P, 1], F32, name="bias")
        streams, gates, values = [], [], []
        for t in range(BLOCKS):
            streams.append(held.tile([P, N], F32, name=f"stream{t}"))
            gates.append(held.tile([P, S], F32, name=f"gates{t}"))
            values.append(held.tile([P, S], F32, name=f"values{t}"))
        for t in range(BLOCKS):
            rows = slice(t * P, (t + 1) * P)
            early = N if t < BLOCKS - 1 else N // 2
            nc.scalar.dma_start(streams[t][:, :early], y[rows, :early])
            nc.sync.dma_start(gates[t][:], tab[1, rows, :])
            nc.sync.dma_start(values[t][:], tab[0, rows, :])
        nc.sync.dma_start(weights[:], w.rearrange("(t p) m -> p t m", p=P))
        nc.sync.dma_start(streams[-1][:, N // 2 :], y[K - P :, N // 2 :])
        nc.sync.dma_start(bias[:], b)

        products = [psum.tile([M, PIECE], F32, name=f"product{c}") for c in range(PIECES)]
        results = [held.tile([M, PIECE], F32, name=f"result{c}") for c in range(PIECES)]
        columns = [slice(c * PIECE, (c + 1) * PIECE) for c in range(PIECES)]
        for t in range(BLOCKS):
            gate = held.tile([P, N], F32, name=f"gate{t}")
            totals = [held.tile([P, PIECE], F32, name=f"total{t}_{c}") for c in range(PIECES)]
            nc.scalar.activation(gate[:], gates[t][:].indirect(offsets[:]), SILU)

            def look_up(c):
                part = offsets[:, c * PIECE // 16 : (c + 1) * PIECE // 16]
                nc.vector.tensor_tensor(totals[c][:], values[t][:].indirect(part), streams[t][:, columns[c]], ADD)

            look_up(0)
            for c in range(PIECES):
                if c + 1 < PIECES:
                    look_up(c + 1)
                x = held.tile([P, PIECE], BF16, name=f"x{t}_{c}")
                nc.vector.tensor_tensor(x[:], totals[c][:], gate[:, columns[c]], MULT)
                nc.tensor.matmul(products[c][:], weights[:, t, :], x[:], start=t == 0, stop=t == BLOCKS - 1)
        for c in range(PIECES):
            nc.scalar.activation(results[c][:], products[c][:], RELU, bias=bias[:])
            nc.sync.dma_start(out[:, columns[c]], results[c][:])
